import numpy as np
import ml_dtypes


def mxq(x, axis, fmt="e4m3"):
    dtype, down = {"e4m3": (ml_dtypes.float8_e4m3fn, 7), "e5m2": (ml_dtypes.float8_e5m2, 14)}[fmt]
    v = np.moveaxis(np.asarray(x, np.float32).astype(ml_dtypes.bfloat16).astype(np.float64), axis, -1)
    blocks = v.reshape(v.shape[:-1] + (-1, 32))
    amax = np.abs(blocks).max(-1, keepdims=True)
    byte = np.maximum(np.where(amax > 0, np.frexp(amax)[1] - 1 + 127, 0) - down, 1)
    scale = np.exp2(byte - 127.0)
    codes = (blocks / scale).astype(np.float32).astype(dtype).astype(np.float64)
    return np.moveaxis((codes * scale).reshape(v.shape), -1, axis)


WIDE = False


def mx_kscale(k):
    if not WIDE:
        return np.ones(k)
    levels = np.array([30, -30])
    if k % 512:
        return np.exp2(np.random.permutation(np.resize(levels, k // 32))).repeat(32)
    a = np.empty((k // 512, 16))
    for p in range(k // 512):
        a[p, :8] = np.random.permutation(np.resize(levels, 8))
        for g in range(8):
            far = levels[np.abs(levels - a[p, g]) >= 10]
            a[p, g + 8] = far[np.random.randint(len(far))]
    return np.exp2(a.ravel()).repeat(32)


def f64(x):
    return np.asarray(x).astype(np.float64)


def striped(idx):
    return np.tile(np.asarray(idx).reshape(-1, 16).T, (8, 1)).astype(np.uint16)


def unstriped(offs):
    return offs[:16].T.reshape(-1).astype(np.int64)


E2M1 = np.array([0.0, 0.5, 1.0, 1.5, 2.0, 3.0, 4.0, 6.0, -0.0, -0.5, -1.0, -1.5, -2.0, -3.0, -4.0, -6.0])


def pack_weight(w, fmt):
    k, n = w.shape
    w = f64(np.asarray(w, np.float32).astype(ml_dtypes.bfloat16)).reshape(k // 32, 32, n)
    amax = np.abs(w).max(1)
    if fmt in ("e4m3", "e5m2"):
        byte = np.frexp(amax)[1] - 1 + 127 - (7 if fmt == "e4m3" else 14)
    else:
        mant, ex = np.frexp(amax / 6.0)
        byte = np.where(mant > 0.5, ex, ex - 1) + 127
    byte = np.clip(np.where(amax > 0, byte, 1), 1, 254)
    scaled = (w * np.exp2(127.0 - byte)[:, None, :]).reshape(k, n).astype(np.float32)
    by_word = np.ascontiguousarray(scaled.reshape(k // 512, 128, 4, n).transpose(0, 1, 3, 2))
    if fmt in ("e4m3", "e5m2"):
        words = by_word.astype(ml_dtypes.float8_e4m3fn if fmt == "e4m3" else ml_dtypes.float8_e5m2).view(np.uint8)
    else:
        c = by_word.astype(ml_dtypes.float4_e2m1fn).view(np.uint8) & 0xF
        words = (c[..., 0::2] | (c[..., 1::2] << 4)).reshape(k // 512, 128, 2 * n)
    return np.ascontiguousarray(words), np.ascontiguousarray(byte.astype(np.uint8).reshape(k // 512, 16, n))


def unpack_weight(words, scales, fmt):
    g, _, n = scales.shape
    words = np.ascontiguousarray(words).reshape(g, 128, n, -1)
    if fmt in ("e4m3", "e5m2"):
        vals = words.view(ml_dtypes.float8_e4m3fn if fmt == "e4m3" else ml_dtypes.float8_e5m2).astype(np.float64)
    else:
        nib = np.empty((g, 128, n, 4), np.uint8)
        nib[..., 0::2] = words & 0xF
        nib[..., 1::2] = words >> 4
        vals = E2M1[nib]
    vals = vals * np.repeat(np.exp2(scales.astype(np.float64) - 127.0), 8, axis=1)[..., None]
    return vals.transpose(0, 1, 3, 2).reshape(g * 512, n)


K, T, J, R, C, V, O, N, S, U = 512, 1024, 256, 512, 512, 1024, 256, 256, 1024, 128


def setup_inputs():
    n = np.random.standard_normal
    idx = np.random.permutation(T)[:J]
    idx2 = np.random.permutation(C)[:J]
    idx3 = np.random.permutation(V)[:C]
    idx4 = np.random.permutation(C)[:O]
    idx5 = np.random.permutation(S)[:N]
    idx6 = np.random.permutation(O)[:U]
    idx7 = np.random.permutation(O)[:U]
    fk = mx_kscale(K)
    fr = mx_kscale(R)
    xtp = pack_weight(n((K, T)) / fk[:, None], "e2m1")
    wp = pack_weight(n((K, R)) * 1 / np.sqrt(K) * fk[:, None] * fr, "e5m2")
    vsp = pack_weight(n((R, S)) * 1 / np.sqrt(R) / fr[:, None], "e4m3")
    return {
        "xt_words": xtp[0],
        "xt_scales": xtp[1],
        "w_words": wp[0],
        "w_scales": wp[1],
        "tb": (np.random.randint(-9, 10, (R, V)).astype(np.float64)).astype(np.float32),
        "st": (np.random.uniform(0.06, 0.24, (R, 1)) * fr[:, None]).astype(np.float32),
        "vs_words": vsp[0],
        "vs_scales": vsp[1],
        "so": (np.random.uniform(0.5, 1.6, (N, 1))).astype(np.float32),
        "offs": striped(idx),
        "offs2": striped(idx2),
        "offs3": striped(idx3),
        "offs4": striped(idx4),
        "offs5": striped(idx5),
        "offs6": striped(idx6),
        "offs7": striped(idx7),
    }


def reference(xt_words, xt_scales, w_words, w_scales, tb, st, vs_words, vs_scales, so, offs, offs2, offs3, offs4, offs5, offs6, offs7):
    idx = unstriped(offs)
    idx2 = unstriped(offs2)
    idx3 = unstriped(offs3)
    idx4 = unstriped(offs4)
    idx5 = unstriped(offs5)
    idx6 = unstriped(offs6)
    idx7 = unstriped(offs7)
    xtu = unpack_weight(xt_words, xt_scales, "e2m1")
    wu = unpack_weight(w_words, w_scales, "e5m2")
    vsu = unpack_weight(vs_words, vs_scales, "e4m3")
    xtidxg = xtu[:, idx]
    a = wu.T @ xtidxg
    pw = np.zeros((R, C))
    pw[:, idx2] = a
    pg = np.abs(pw - f64(tb)[:, idx3] * f64(st))
    hid = pg[:, idx4]
    vsidx5g = vsu[:, idx5]
    hidq = mxq(hid, 0, "e5m2")
    p = vsidx5g.T @ hidq
    y = p[:, idx6] - p[:, idx7] * f64(so)
    return y

@@ -1,0 +1,174 @@
+from contextlib import ExitStack
+
+import concourse.mybir as mybir
+
+K, T, J, R, C, V, O, N, S, U = 512, 1024, 256, 512, 512, 1024, 256, 256, 1024, 128
+FLOPS = 2 * K * R * J + 2 * R * N * O
+
+F32 = mybir.dt.float32
+BF16 = mybir.dt.bfloat16
+I32 = mybir.dt.int32
+U32 = mybir.dt.uint32
+U16 = mybir.dt.uint16
+U8 = mybir.dt.uint8
+E2M1 = mybir.dt.float4_e2m1fn_x4
+E4M3 = mybir.dt.float8_e4m3fn_x4
+E5M2 = mybir.dt.float8_e5m2_x4
+ACT = mybir.ActivationFunctionType
+ALU = mybir.AluOpType
+
+P = 128
+PACK = 4
+QUADS = 4
+QUAD = 32
+
+
+def tile_list_stampedsteps_solo_store_weighedout_kernel(
+    tc, xt_words, xt_scales, w_words, w_scales, tb, st, vs_words, vs_scales, so,
+    offs, offs2, offs3, offs4, offs5, offs6, offs7, out,
+):
+    nc = tc.nc
+    with ExitStack() as ctx:
+        sb = ctx.enter_context(tc.tile_pool(name="sb", bufs=1))
+        ps = ctx.enter_context(tc.psum_pool(name="ps", bufs=1))
+
+        def sbuf(name, shape, dtype, tag=None):
+            return sb.tile(shape, dtype, name=name, tag=tag or name, align_bytes=64)
+
+        def load_list(name, src):
+            lst = sbuf(name, list(src.shape), U16)
+            nc.sync.dma_start(lst[:], src)
+            return lst
+
+        def load_scale_rows(queue, plane, scales):
+            rows = scales[0].bitcast(I32)
+            for q in range(QUADS):
+                queue.dma_start(plane[QUAD * q : QUAD * q + PACK, :].bitcast(I32), rows[PACK * q : PACK * (q + 1), :])
+
+        xt_plane = sbuf("xt_plane", [P, T], U8)
+        nc.gpsimd.memset(xt_plane[:].bitcast(I32), 0)
+        vs_plane = sbuf("vs_plane", [P, S], U8)
+        nc.vector.memset(vs_plane[:].bitcast(I32), 0)
+
+        tb_rows = tb.rearrange("(p t) v -> t p v", t=PACK)
+        tb_sb = [sbuf("tb%d" % t, [P, V], F32) for t in range(PACK)]
+        w_rows = sbuf("w_rows", [PACK, QUADS, R // 4], I32)
+        nc.sync.dma_start(w_rows[:], w_scales[0].bitcast(I32).rearrange("(q r) c -> r q c", r=PACK))
+        tok_list = load_list("tok_list", offs)
+        load_scale_rows(nc.scalar, xt_plane, xt_scales)
+        xt_sb = sbuf("xt_sb", [P, T], U16)
+        nc.sync.dma_start(xt_sb[:].bitcast(I32), xt_words[0].bitcast(I32))
+        w_sb = sbuf("w_sb", [P, R], U32)
+        nc.sync.dma_start(w_sb[:].bitcast(I32), w_words[0].rearrange("p n t -> p (n t)").bitcast(I32))
+        nc.sync.dma_start(tb_sb[0][:], tb_rows[0])
+        base_list = load_list("base_list", offs3)
+        st_sb = sbuf("st_sb", [P, PACK], F32)
+        nc.sync.dma_start(st_sb[:], st.rearrange("(p t) o -> p (t o)", t=PACK))
+        put_list = load_list("put_list", offs2)
+        for t in range(1, PACK):
+            nc.sync.dma_start(tb_sb[t][:], tb_rows[t])
+        load_scale_rows(nc.sync, vs_plane, vs_scales)
+        store_list = load_list("store_list", offs5)
+        vs_sb = sbuf("vs_sb", [P, S], U32)
+        nc.sync.dma_start(vs_sb[:].bitcast(I32), vs_words[0].rearrange("p n t -> p (n t)").bitcast(I32))
+        read_list = load_list("read_list", offs4)
+        first_list = load_list("first_list", offs6)
+        second_list = load_list("second_list", offs7)
+        so_sb = sbuf("so_sb", [P, N // P], F32)
+        with nc.allow_non_contiguous_dma(reason="one weight to a partition"):
+            nc.sync.dma_start(so_sb[:], so.rearrange("(h p) o -> p (h o)", p=P))
+
+        boards = [sbuf("board%d" % t, [P, C], F32) for t in range(PACK)]
+        for t in range(PACK):
+            nc.gpsimd.memset(boards[t][:], 0.0)
+
+        w_plane = sbuf("w_plane", [P, R], U8)
+        nc.vector.memset(w_plane[:].bitcast(I32), 0)
+        for q in range(QUADS):
+            nc.vector.tensor_copy(w_plane[QUAD * q : QUAD * q + PACK, :].bitcast(I32), w_rows[:, q, :])
+        xt_g = sbuf("xt_g", [P, J], U16)
+        nc.vector.tensor_copy(xt_g[:], xt_sb[:].indirect(tok_list[:]))
+        xt_plane_g = sbuf("xt_plane_g", [P, J], U8)
+        nc.vector.tensor_copy(xt_plane_g[:], xt_plane[:].indirect(tok_list[:]))
+        w_plane_t = sbuf("w_plane_t", [P, PACK, P], U8)
+        nc.gpsimd.tensor_copy(w_plane_t[:], w_plane[:].rearrange("p (m t) -> p t m", t=PACK))
+        w_t = sbuf("w_t", [P, PACK, P], U32)
+        w_by_t = w_sb[:].rearrange("p (m t) -> p m t", t=PACK)
+        nc.scalar.copy(w_t[:, 0, :], w_by_t[:, :, 0])
+        nc.scalar.copy(w_t[:, 1:, :].rearrange("p t m -> p m t"), w_by_t[:, :, 1:])
+
+        a_ps = [ps.tile([P, J], F32, name="a_ps%d" % t) for t in range(PACK)]
+        for t in (0, 1, 3, 2):
+            nc.tensor.matmul_mx(
+                a_ps[t][:], lhsT=w_t[:, t, :].bitcast(E5M2), lhsT_scale=w_plane_t[:, t, :],
+                rhs=xt_g[:].bitcast(E2M1), rhs_scale=xt_plane_g[:], start=True, stop=True,
+            )
+
+        a_sb = [sbuf("a_sb%d" % t, [P, J], F32, "tb0" if t == 2 else None) for t in range(PACK)]
+        base = [sbuf("base%d" % t, [P, C], F32) for t in range(PACK)]
+        diff = [sbuf("diff%d" % t, [P, C], F32, "vs_plane" if t == 3 else None) for t in range(PACK)]
+        kept_on = ["a_sb3", "tb3", "diff1", "diff2"]
+        kept = [sbuf("kept%d" % t, [P, C], F32, kept_on[t]) for t in range(PACK)]
+        hid = sbuf("hid", [P, PACK, O], F32)
+        vs_g = sbuf("vs_g", [P, N], U32)
+        vs_plane_g = sbuf("vs_plane_g", [P, N], U8)
+
+        def fetch_base(t):
+            nc.scalar.activation(base[t][:], tb_sb[t][:].indirect(base_list[:]), ACT.Copy, scale=st_sb[:, t : t + 1])
+
+        fetch_base(0)
+        for t in (0, 1, 3):
+            nc.vector.tensor_copy(a_sb[t][:], a_ps[t][:])
+            nc.vector.tensor_copy(boards[t][:].indirect(put_list[:]), a_sb[t][:])
+        nc.scalar.copy(a_sb[2][:], a_ps[2][:])
+        nc.scalar.activation(boards[2][:].indirect(put_list[:]), a_sb[2][:], ACT.Copy)
+        for t in range(1, PACK):
+            fetch_base(t)
+        for t in range(PACK - 1):
+            nc.gpsimd.tensor_tensor(diff[t][:], boards[t][:], base[t][:], ALU.subtract)
+        nc.vector.tensor_reduce(
+            kept[0][:], diff[0][:].unsqueeze(2), mybir.AxisListType.X, ALU.max, apply_absolute_value=True, opt_input=False,
+        )
+        nc.vector.tensor_copy(vs_plane_g[:], vs_plane[:].indirect(store_list[:]))
+        nc.vector.tensor_tensor(diff[3][:], boards[3][:], base[3][:], ALU.subtract)
+        nc.vector.tensor_copy(vs_g[:], vs_sb[:].indirect(store_list[:]))
+        for t in range(1, PACK):
+            nc.scalar.activation(kept[t][:], diff[t][:], ACT.Abs)
+        for t in (0, 3):
+            nc.vector.tensor_copy(hid[:, t, :], kept[t][:].indirect(read_list[:]))
+        for t in (1, 2):
+            nc.scalar.activation(hid[:, t, :], kept[t][:].indirect(read_list[:]), ACT.Copy)
+
+        halves = N // P
+        hid_bf = sbuf("hid_bf", [P, O, PACK], BF16)
+        hid_q = sbuf("hid_q", [P, O], U32)
+        hid_plane = sbuf("hid_plane", [P, O], U8)
+        reads = [slice(P * g, P * (g + 1)) for g in range(O // P)]
+        for cols in reads:
+            nc.vector.tensor_copy(hid_bf[:, cols, :], hid[:, :, cols].rearrange("p t o -> p o t"))
+        for cols in reads:
+            nc.vector.quantize_mx(
+                hid_q[:, cols].bitcast(E5M2), hid_plane[:, cols], hid_bf[:, cols, :].rearrange("p o t -> p (o t)"),
+            )
+
+        p_sb = [sbuf("p_sb%d" % h, [P, O], F32) for h in range(halves)]
+        first = sbuf("first", [P, halves, U], F32)
+        second = sbuf("second", [P, halves, U], F32)
+        y = sbuf("y", [P, halves, U], F32)
+        for g, cols in enumerate(reads):
+            for h in range(halves):
+                feats = slice(P * h, P * (h + 1))
+                p_ps = ps.tile([P, P], F32, name="p_ps%d%d" % (g, h))
+                nc.tensor.matmul_mx(
+                    p_ps[:], lhsT=vs_g[:, feats].bitcast(E4M3), lhsT_scale=vs_plane_g[:, feats],
+                    rhs=hid_q[:, cols].bitcast(E5M2), rhs_scale=hid_plane[:, cols], start=True, stop=True,
+                )
+                if (g, h) == (1, 0):
+                    nc.vector.tensor_copy(p_sb[h][:, cols], p_ps[:])
+                else:
+                    nc.scalar.copy(p_sb[h][:, cols], p_ps[:])
+        for h in range(halves):
+            nc.vector.tensor_copy(first[:, h, :], p_sb[h][:].indirect(first_list[:]))
+            nc.scalar.activation(second[:, h, :], p_sb[h][:].indirect(second_list[:]), ACT.Copy, scale=so_sb[:, h : h + 1])
+        nc.vector.tensor_tensor(y[:], first[:], second[:], ALU.subtract)
+        nc.sync.dma_start(out.rearrange("(h p) u -> p h u", p=P), y[:])

@@ -80,35 +80,37 @@ def tile_list_stampedsteps_solo_store_weighedout_kernel(
 
         boards = [sbuf("board%d" % t, [P, C], F32) for t in range(PACK)]
         for t in range(PACK):
-            nc.gpsimd.memset(boards[t][:], 0.0)
+            (nc.gpsimd if t < 2 else nc.vector).memset(boards[t][:], 0.0)
 
         w_plane = sbuf("w_plane", [P, R], U8)
         nc.vector.memset(w_plane[:].bitcast(I32), 0)
         for q in range(QUADS):
             nc.vector.tensor_copy(w_plane[QUAD * q : QUAD * q + PACK, :].bitcast(I32), w_rows[:, q, :])
+        w_plane_t = sbuf("w_plane_t", [P, PACK, P], U8)
+        nc.vector.tensor_copy(w_plane_t[:], w_plane[:].rearrange("p (m t) -> p t m", t=PACK))
         xt_g = sbuf("xt_g", [P, J], U16)
         nc.vector.tensor_copy(xt_g[:], xt_sb[:].indirect(tok_list[:]))
         xt_plane_g = sbuf("xt_plane_g", [P, J], U8)
         nc.vector.tensor_copy(xt_plane_g[:], xt_plane[:].indirect(tok_list[:]))
-        w_plane_t = sbuf("w_plane_t", [P, PACK, P], U8)
-        nc.gpsimd.tensor_copy(w_plane_t[:], w_plane[:].rearrange("p (m t) -> p t m", t=PACK))
         w_t = sbuf("w_t", [P, PACK, P], U32)
         w_by_t = w_sb[:].rearrange("p (m t) -> p m t", t=PACK)
-        nc.scalar.copy(w_t[:, 0, :], w_by_t[:, :, 0])
-        nc.scalar.copy(w_t[:, 1:, :].rearrange("p t m -> p m t"), w_by_t[:, :, 1:])
+        order = (3, 0, 1, 2)
+        for t in order[:2]:
+            nc.scalar.copy(w_t[:, t, :], w_by_t[:, :, t])
+        nc.scalar.copy(w_t[:, 1:3, :].rearrange("p t m -> p m t"), w_by_t[:, :, 1:3])
 
         a_ps = [ps.tile([P, J], F32, name="a_ps%d" % t) for t in range(PACK)]
-        for t in (0, 1, 3, 2):
+        for t in order:
             nc.tensor.matmul_mx(
                 a_ps[t][:], lhsT=w_t[:, t, :].bitcast(E5M2), lhsT_scale=w_plane_t[:, t, :],
                 rhs=xt_g[:].bitcast(E2M1), rhs_scale=xt_plane_g[:], start=True, stop=True,
             )
 
-        a_sb = [sbuf("a_sb%d" % t, [P, J], F32, "tb0" if t == 2 else None) for t in range(PACK)]
+        last = PACK - 1
+        a_sb = [sbuf("a_sb%d" % t, [P, J], F32) for t in range(PACK)]
         base = [sbuf("base%d" % t, [P, C], F32) for t in range(PACK)]
-        diff = [sbuf("diff%d" % t, [P, C], F32, "vs_plane" if t == 3 else None) for t in range(PACK)]
-        kept_on = ["a_sb3", "tb3", "diff1", "diff2"]
-        kept = [sbuf("kept%d" % t, [P, C], F32, kept_on[t]) for t in range(PACK)]
+        diff = [sbuf("diff%d" % t, [P, C], F32) for t in range(PACK)]
+        kept = [sbuf("kept%d" % t, [P, C], F32, "diff%d" % (t - 1) if t else "tb%d" % last) for t in range(PACK)]
         hid = sbuf("hid", [P, PACK, O], F32)
         vs_g = sbuf("vs_g", [P, N], U32)
         vs_plane_g = sbuf("vs_plane_g", [P, N], U8)
@@ -117,27 +119,23 @@ def tile_list_stampedsteps_solo_store_weighedout_kernel(
             nc.scalar.activation(base[t][:], tb_sb[t][:].indirect(base_list[:]), ACT.Copy, scale=st_sb[:, t : t + 1])
 
         fetch_base(0)
-        for t in (0, 1, 3):
+        for t in order:
             nc.vector.tensor_copy(a_sb[t][:], a_ps[t][:])
+        nc.scalar.activation(boards[last][:].indirect(put_list[:]), a_sb[last][:], ACT.Copy)
+        for t in range(last):
             nc.vector.tensor_copy(boards[t][:].indirect(put_list[:]), a_sb[t][:])
-        nc.scalar.copy(a_sb[2][:], a_ps[2][:])
-        nc.scalar.activation(boards[2][:].indirect(put_list[:]), a_sb[2][:], ACT.Copy)
         for t in range(1, PACK):
             fetch_base(t)
-        for t in range(PACK - 1):
-            nc.gpsimd.tensor_tensor(diff[t][:], boards[t][:], base[t][:], ALU.subtract)
-        nc.vector.tensor_reduce(
-            kept[0][:], diff[0][:].unsqueeze(2), mybir.AxisListType.X, ALU.max, apply_absolute_value=True, opt_input=False,
-        )
+        for t in range(PACK):
+            nc.vector.tensor_tensor(diff[t][:], boards[t][:], base[t][:], ALU.subtract)
         nc.vector.tensor_copy(vs_plane_g[:], vs_plane[:].indirect(store_list[:]))
-        nc.vector.tensor_tensor(diff[3][:], boards[3][:], base[3][:], ALU.subtract)
         nc.vector.tensor_copy(vs_g[:], vs_sb[:].indirect(store_list[:]))
-        for t in range(1, PACK):
+        for t in range(PACK):
             nc.scalar.activation(kept[t][:], diff[t][:], ACT.Abs)
-        for t in (0, 3):
-            nc.vector.tensor_copy(hid[:, t, :], kept[t][:].indirect(read_list[:]))
-        for t in (1, 2):
+        for t in (0, 1):
             nc.scalar.activation(hid[:, t, :], kept[t][:].indirect(read_list[:]), ACT.Copy)
+        for t in (2, 3):
+            nc.vector.tensor_copy(hid[:, t, :], kept[t][:].indirect(read_list[:]))
 
         halves = N // P
         hid_bf = sbuf("hid_bf", [P, O, PACK], BF16)
@@ -145,7 +143,10 @@ def tile_list_stampedsteps_solo_store_weighedout_kernel(
         hid_plane = sbuf("hid_plane", [P, O], U8)
         reads = [slice(P * g, P * (g + 1)) for g in range(O // P)]
         for cols in reads:
-            nc.vector.tensor_copy(hid_bf[:, cols, :], hid[:, :, cols].rearrange("p t o -> p o t"))
+            nc.vector.tensor_copy(
+                hid_bf[:, cols, :].rearrange("p (c i) t -> p c t i", i=PACK),
+                hid[:, :, cols].rearrange("p t (c i) -> p c t i", i=PACK),
+            )
         for cols in reads:
             nc.vector.quantize_mx(
                 hid_q[:, cols].bitcast(E5M2), hid_plane[:, cols], hid_bf[:, cols, :].rearrange("p o t -> p (o t)"),
@@ -163,12 +164,13 @@ def tile_list_stampedsteps_solo_store_weighedout_kernel(
                     p_ps[:], lhsT=vs_g[:, feats].bitcast(E4M3), lhsT_scale=vs_plane_g[:, feats],
                     rhs=hid_q[:, cols].bitcast(E5M2), rhs_scale=hid_plane[:, cols], start=True, stop=True,
                 )
-                if (g, h) == (1, 0):
+                if (g, h) == (1, 1):
                     nc.vector.tensor_copy(p_sb[h][:, cols], p_ps[:])
                 else:
                     nc.scalar.copy(p_sb[h][:, cols], p_ps[:])
         for h in range(halves):
             nc.vector.tensor_copy(first[:, h, :], p_sb[h][:].indirect(first_list[:]))
             nc.scalar.activation(second[:, h, :], p_sb[h][:].indirect(second_list[:]), ACT.Copy, scale=so_sb[:, h : h + 1])
-        nc.vector.tensor_tensor(y[:], first[:], second[:], ALU.subtract)
-        nc.sync.dma_start(out.rearrange("(h p) u -> p h u", p=P), y[:])
+        for h in range(halves):
+            nc.vector.tensor_tensor(y[:, h, :], first[:, h, :], second[:, h, :], ALU.subtract)
+            nc.sync.dma_start(out[P * h : P * (h + 1), :], y[:, h, :])

@@ -47,8 +47,6 @@ def tile_list_stampedsteps_solo_store_weighedout_kernel(
 
         xt_plane = sbuf("xt_plane", [P, T], U8)
         nc.gpsimd.memset(xt_plane[:].bitcast(I32), 0)
-        vs_plane = sbuf("vs_plane", [P, S], U8)
-        nc.vector.memset(vs_plane[:].bitcast(I32), 0)
 
         tb_rows = tb.rearrange("(p t) v -> t p v", t=PACK)
         tb_sb = [sbuf("tb%d" % t, [P, V], F32) for t in range(PACK)]
@@ -67,11 +65,10 @@ def tile_list_stampedsteps_solo_store_weighedout_kernel(
         put_list = load_list("put_list", offs2)
         for t in range(1, PACK):
             nc.sync.dma_start(tb_sb[t][:], tb_rows[t])
-        load_scale_rows(nc.sync, vs_plane, vs_scales)
         store_list = load_list("store_list", offs5)
+        read_list = load_list("read_list", offs4)
         vs_sb = sbuf("vs_sb", [P, S], U32)
         nc.sync.dma_start(vs_sb[:].bitcast(I32), vs_words[0].rearrange("p n t -> p (n t)").bitcast(I32))
-        read_list = load_list("read_list", offs4)
         first_list = load_list("first_list", offs6)
         second_list = load_list("second_list", offs7)
         so_sb = sbuf("so_sb", [P, N // P], F32)
@@ -80,24 +77,27 @@ def tile_list_stampedsteps_solo_store_weighedout_kernel(
 
         boards = [sbuf("board%d" % t, [P, C], F32) for t in range(PACK)]
         for t in range(PACK):
-            (nc.gpsimd if t < 2 else nc.vector).memset(boards[t][:], 0.0)
+            nc.gpsimd.memset(boards[t][:], 0.0)
 
         w_plane = sbuf("w_plane", [P, R], U8)
         nc.vector.memset(w_plane[:].bitcast(I32), 0)
         for q in range(QUADS):
             nc.vector.tensor_copy(w_plane[QUAD * q : QUAD * q + PACK, :].bitcast(I32), w_rows[:, q, :])
-        w_plane_t = sbuf("w_plane_t", [P, PACK, P], U8)
-        nc.vector.tensor_copy(w_plane_t[:], w_plane[:].rearrange("p (m t) -> p t m", t=PACK))
         xt_g = sbuf("xt_g", [P, J], U16)
         nc.vector.tensor_copy(xt_g[:], xt_sb[:].indirect(tok_list[:]))
         xt_plane_g = sbuf("xt_plane_g", [P, J], U8)
         nc.vector.tensor_copy(xt_plane_g[:], xt_plane[:].indirect(tok_list[:]))
+        w_plane_t = sbuf("w_plane_t", [P, PACK, P], U8)
+        nc.gpsimd.tensor_copy(w_plane_t[:], w_plane[:].rearrange("p (m t) -> p t m", t=PACK))
+        vs_plane = sbuf("vs_plane", [P, S], U8, "w_plane")
+        nc.gpsimd.memset(vs_plane[:].bitcast(I32), 0)
+        load_scale_rows(nc.gpsimd, vs_plane, vs_scales)
         w_t = sbuf("w_t", [P, PACK, P], U32)
         w_by_t = w_sb[:].rearrange("p (m t) -> p m t", t=PACK)
-        order = (3, 0, 1, 2)
+        order = (1, 0, 2, 3)
         for t in order[:2]:
             nc.scalar.copy(w_t[:, t, :], w_by_t[:, :, t])
-        nc.scalar.copy(w_t[:, 1:3, :].rearrange("p t m -> p m t"), w_by_t[:, :, 1:3])
+        nc.scalar.copy(w_t[:, 2:, :].rearrange("p t m -> p m t"), w_by_t[:, :, 2:])
 
         a_ps = [ps.tile([P, J], F32, name="a_ps%d" % t) for t in range(PACK)]
         for t in order:
@@ -109,59 +109,67 @@ def tile_list_stampedsteps_solo_store_weighedout_kernel(
         last = PACK - 1
         a_sb = [sbuf("a_sb%d" % t, [P, J], F32) for t in range(PACK)]
         base = [sbuf("base%d" % t, [P, C], F32) for t in range(PACK)]
-        diff = [sbuf("diff%d" % t, [P, C], F32) for t in range(PACK)]
-        kept = [sbuf("kept%d" % t, [P, C], F32, "diff%d" % (t - 1) if t else "tb%d" % last) for t in range(PACK)]
+        diff = [sbuf("diff%d" % t, [P, C], F32, "tb2" if t == last else None) for t in range(PACK)]
+        kept = [sbuf("kept%d" % t, [P, C], F32, ("tb2", "w_plane", None, None)[t]) for t in range(PACK)]
         hid = sbuf("hid", [P, PACK, O], F32)
-        vs_g = sbuf("vs_g", [P, N], U32)
         vs_plane_g = sbuf("vs_plane_g", [P, N], U8)
 
         def fetch_base(t):
             nc.scalar.activation(base[t][:], tb_sb[t][:].indirect(base_list[:]), ACT.Copy, scale=st_sb[:, t : t + 1])
 
+        def magnitude(t):
+            nc.scalar.activation(kept[t][:], diff[t][:], ACT.Abs)
+
+        def read(t):
+            nc.vector.tensor_copy(hid[:, t, :], kept[t][:].indirect(read_list[:]))
+
         fetch_base(0)
         for t in order:
             nc.vector.tensor_copy(a_sb[t][:], a_ps[t][:])
-        nc.scalar.activation(boards[last][:].indirect(put_list[:]), a_sb[last][:], ACT.Copy)
-        for t in range(last):
+        nc.scalar.activation(boards[1][:].indirect(put_list[:]), a_sb[1][:], ACT.Copy)
+        for t in order[1:]:
             nc.vector.tensor_copy(boards[t][:].indirect(put_list[:]), a_sb[t][:])
         for t in range(1, PACK):
             fetch_base(t)
-        for t in range(PACK):
-            nc.vector.tensor_tensor(diff[t][:], boards[t][:], base[t][:], ALU.subtract)
+        for t in range(last):
+            nc.gpsimd.tensor_tensor(diff[t][:], boards[t][:], base[t][:], ALU.subtract)
         nc.vector.tensor_copy(vs_plane_g[:], vs_plane[:].indirect(store_list[:]))
-        nc.vector.tensor_copy(vs_g[:], vs_sb[:].indirect(store_list[:]))
-        for t in range(PACK):
-            nc.scalar.activation(kept[t][:], diff[t][:], ACT.Abs)
-        for t in (0, 1):
-            nc.scalar.activation(hid[:, t, :], kept[t][:].indirect(read_list[:]), ACT.Copy)
-        for t in (2, 3):
-            nc.vector.tensor_copy(hid[:, t, :], kept[t][:].indirect(read_list[:]))
+        magnitude(0)
+        read(0)
+        nc.vector.tensor_tensor(diff[last][:], boards[last][:], base[last][:], ALU.subtract)
+        for t in range(1, PACK):
+            magnitude(t)
+        for t in range(1, last):
+            read(t)
+        nc.vector.tensor_copy(hid[:, last, :P], kept[last][:].indirect(read_list[:, : P // 16]))
+        nc.scalar.activation(hid[:, last, P:], kept[last][:].indirect(read_list[:, P // 16 :]), ACT.Copy)
 
         halves = N // P
         hid_bf = sbuf("hid_bf", [P, O, PACK], BF16)
         hid_q = sbuf("hid_q", [P, O], U32)
         hid_plane = sbuf("hid_plane", [P, O], U8)
+        vs_g = [sbuf("vs_g%d" % h, [P, P], U32, ("hid", "hid_bf")[h]) for h in range(halves)]
         reads = [slice(P * g, P * (g + 1)) for g in range(O // P)]
         for cols in reads:
             nc.vector.tensor_copy(
                 hid_bf[:, cols, :].rearrange("p (c i) t -> p c t i", i=PACK),
                 hid[:, :, cols].rearrange("p t (c i) -> p c t i", i=PACK),
             )
-        for cols in reads:
+        for g, cols in enumerate(reads):
             nc.vector.quantize_mx(
                 hid_q[:, cols].bitcast(E5M2), hid_plane[:, cols], hid_bf[:, cols, :].rearrange("p o t -> p (o t)"),
             )
+            nc.vector.tensor_copy(vs_g[g][:], vs_sb[:].indirect(store_list[:, P // 16 * g : P // 16 * (g + 1)]))
 
         p_sb = [sbuf("p_sb%d" % h, [P, O], F32) for h in range(halves)]
         first = sbuf("first", [P, halves, U], F32)
         second = sbuf("second", [P, halves, U], F32)
         y = sbuf("y", [P, halves, U], F32)
-        for g, cols in enumerate(reads):
-            for h in range(halves):
-                feats = slice(P * h, P * (h + 1))
+        for h in range(halves):
+            for g, cols in enumerate(reads):
                 p_ps = ps.tile([P, P], F32, name="p_ps%d%d" % (g, h))
                 nc.tensor.matmul_mx(
-                    p_ps[:], lhsT=vs_g[:, feats].bitcast(E4M3), lhsT_scale=vs_plane_g[:, feats],
+                    p_ps[:], lhsT=vs_g[h][:].bitcast(E4M3), lhsT_scale=vs_plane_g[:, P * h : P * (h + 1)],
                     rhs=hid_q[:, cols].bitcast(E5M2), rhs_scale=hid_plane[:, cols], start=True, stop=True,
                 )
                 if (g, h) == (1, 1):

from contextlib import ExitStack

import concourse.mybir as mybir

K, T, J, R, C, V, O, N, S, U = 512, 1024, 256, 512, 512, 1024, 256, 256, 1024, 128
FLOPS = 2 * K * R * J + 2 * R * N * O

F32 = mybir.dt.float32
BF16 = mybir.dt.bfloat16
I32 = mybir.dt.int32
U32 = mybir.dt.uint32
U16 = mybir.dt.uint16
U8 = mybir.dt.uint8
E2M1 = mybir.dt.float4_e2m1fn_x4
E4M3 = mybir.dt.float8_e4m3fn_x4
E5M2 = mybir.dt.float8_e5m2_x4
ACT = mybir.ActivationFunctionType
ALU = mybir.AluOpType

P = 128
PACK = 4
QUADS = 4
QUAD = 32


def tile_list_stampedsteps_solo_store_weighedout_kernel(
    tc, xt_words, xt_scales, w_words, w_scales, tb, st, vs_words, vs_scales, so,
    offs, offs2, offs3, offs4, offs5, offs6, offs7, out,
):
    nc = tc.nc
    with ExitStack() as ctx:
        sb = ctx.enter_context(tc.tile_pool(name="sb", bufs=1))
        ps = ctx.enter_context(tc.psum_pool(name="ps", bufs=1))

        def sbuf(name, shape, dtype, tag=None):
            return sb.tile(shape, dtype, name=name, tag=tag or name, align_bytes=64)

        def load_list(name, src):
            lst = sbuf(name, list(src.shape), U16)
            nc.sync.dma_start(lst[:], src)
            return lst

        def load_scale_rows(queue, plane, scales):
            rows = scales[0].bitcast(I32)
            for q in range(QUADS):
                queue.dma_start(plane[QUAD * q : QUAD * q + PACK, :].bitcast(I32), rows[PACK * q : PACK * (q + 1), :])

        xt_plane = sbuf("xt_plane", [P, T], U8)
        nc.gpsimd.memset(xt_plane[:].bitcast(I32), 0)

        tb_rows = tb.rearrange("(p t) v -> t p v", t=PACK)
        tb_sb = [sbuf("tb%d" % t, [P, V], F32) for t in range(PACK)]
        w_rows = sbuf("w_rows", [PACK, QUADS, R // 4], I32)
        nc.sync.dma_start(w_rows[:], w_scales[0].bitcast(I32).rearrange("(q r) c -> r q c", r=PACK))
        tok_list = load_list("tok_list", offs)
        load_scale_rows(nc.scalar, xt_plane, xt_scales)
        xt_sb = sbuf("xt_sb", [P, T], U16)
        nc.sync.dma_start(xt_sb[:].bitcast(I32), xt_words[0].bitcast(I32))
        w_sb = sbuf("w_sb", [P, R], U32)
        nc.sync.dma_start(w_sb[:].bitcast(I32), w_words[0].rearrange("p n t -> p (n t)").bitcast(I32))
        nc.sync.dma_start(tb_sb[0][:], tb_rows[0])
        base_list = load_list("base_list", offs3)
        st_sb = sbuf("st_sb", [P, PACK], F32)
        nc.sync.dma_start(st_sb[:], st.rearrange("(p t) o -> p (t o)", t=PACK))
        put_list = load_list("put_list", offs2)
        for t in range(1, PACK):
            nc.sync.dma_start(tb_sb[t][:], tb_rows[t])
        store_list = load_list("store_list", offs5)
        read_list = load_list("read_list", offs4)
        vs_sb = sbuf("vs_sb", [P, S], U32)
        nc.sync.dma_start(vs_sb[:].bitcast(I32), vs_words[0].rearrange("p n t -> p (n t)").bitcast(I32))
        first_list = load_list("first_list", offs6)
        second_list = load_list("second_list", offs7)
        so_sb = sbuf("so_sb", [P, N // P], F32)
        with nc.allow_non_contiguous_dma(reason="one weight to a partition"):
            nc.sync.dma_start(so_sb[:], so.rearrange("(h p) o -> p (h o)", p=P))

        boards = [sbuf("board%d" % t, [P, C], F32) for t in range(PACK)]
        for t in range(PACK):
            nc.gpsimd.memset(boards[t][:], 0.0)

        w_plane = sbuf("w_plane", [P, R], U8)
        nc.vector.memset(w_plane[:].bitcast(I32), 0)
        for q in range(QUADS):
            nc.vector.tensor_copy(w_plane[QUAD * q : QUAD * q + PACK, :].bitcast(I32), w_rows[:, q, :])
        xt_g = sbuf("xt_g", [P, J], U16)
        nc.vector.tensor_copy(xt_g[:], xt_sb[:].indirect(tok_list[:]))
        xt_plane_g = sbuf("xt_plane_g", [P, J], U8)
        nc.vector.tensor_copy(xt_plane_g[:], xt_plane[:].indirect(tok_list[:]))
        w_plane_t = sbuf("w_plane_t", [P, PACK, P], U8)
        nc.gpsimd.tensor_copy(w_plane_t[:], w_plane[:].rearrange("p (m t) -> p t m", t=PACK))
        vs_plane = sbuf("vs_plane", [P, S], U8, "w_plane")
        nc.gpsimd.memset(vs_plane[:].bitcast(I32), 0)
        load_scale_rows(nc.gpsimd, vs_plane, vs_scales)
        w_t = sbuf("w_t", [P, PACK, P], U32)
        w_by_t = w_sb[:].rearrange("p (m t) -> p m t", t=PACK)
        order = (1, 0, 2, 3)
        for t in order[:2]:
            nc.scalar.copy(w_t[:, t, :], w_by_t[:, :, t])
        nc.scalar.copy(w_t[:, 2:, :].rearrange("p t m -> p m t"), w_by_t[:, :, 2:])

        a_ps = [ps.tile([P, J], F32, name="a_ps%d" % t) for t in range(PACK)]
        for t in order:
            nc.tensor.matmul_mx(
                a_ps[t][:], lhsT=w_t[:, t, :].bitcast(E5M2), lhsT_scale=w_plane_t[:, t, :],
                rhs=xt_g[:].bitcast(E2M1), rhs_scale=xt_plane_g[:], start=True, stop=True,
            )

        last = PACK - 1
        a_sb = [sbuf("a_sb%d" % t, [P, J], F32) for t in range(PACK)]
        base = [sbuf("base%d" % t, [P, C], F32) for t in range(PACK)]
        diff = [sbuf("diff%d" % t, [P, C], F32, "tb2" if t == last else None) for t in range(PACK)]
        kept = [sbuf("kept%d" % t, [P, C], F32, ("tb2", "w_plane", None, None)[t]) for t in range(PACK)]
        hid = sbuf("hid", [P, PACK, O], F32)
        vs_plane_g = sbuf("vs_plane_g", [P, N], U8)

        def fetch_base(t):
            nc.scalar.activation(base[t][:], tb_sb[t][:].indirect(base_list[:]), ACT.Copy, scale=st_sb[:, t : t + 1])

        def magnitude(t):
            nc.scalar.activation(kept[t][:], diff[t][:], ACT.Abs)

        def read(t):
            nc.vector.tensor_copy(hid[:, t, :], kept[t][:].indirect(read_list[:]))

        fetch_base(0)
        for t in order:
            nc.vector.tensor_copy(a_sb[t][:], a_ps[t][:])
        nc.scalar.activation(boards[1][:].indirect(put_list[:]), a_sb[1][:], ACT.Copy)
        for t in order[1:]:
            nc.vector.tensor_copy(boards[t][:].indirect(put_list[:]), a_sb[t][:])
        for t in range(1, PACK):
            fetch_base(t)
        for t in range(last):
            nc.gpsimd.tensor_tensor(diff[t][:], boards[t][:], base[t][:], ALU.subtract)
        nc.vector.tensor_copy(vs_plane_g[:], vs_plane[:].indirect(store_list[:]))
        magnitude(0)
        read(0)
        nc.vector.tensor_tensor(diff[last][:], boards[last][:], base[last][:], ALU.subtract)
        for t in range(1, PACK):
            magnitude(t)
        for t in range(1, last):
            read(t)
        nc.vector.tensor_copy(hid[:, last, :P], kept[last][:].indirect(read_list[:, : P // 16]))
        nc.scalar.activation(hid[:, last, P:], kept[last][:].indirect(read_list[:, P // 16 :]), ACT.Copy)

        halves = N // P
        hid_bf = sbuf("hid_bf", [P, O, PACK], BF16)
        hid_q = sbuf("hid_q", [P, O], U32)
        hid_plane = sbuf("hid_plane", [P, O], U8)
        vs_g = [sbuf("vs_g%d" % h, [P, P], U32, ("hid", "hid_bf")[h]) for h in range(halves)]
        reads = [slice(P * g, P * (g + 1)) for g in range(O // P)]
        for cols in reads:
            nc.vector.tensor_copy(
                hid_bf[:, cols, :].rearrange("p (c i) t -> p c t i", i=PACK),
                hid[:, :, cols].rearrange("p t (c i) -> p c t i", i=PACK),
            )
        for g, cols in enumerate(reads):
            nc.vector.quantize_mx(
                hid_q[:, cols].bitcast(E5M2), hid_plane[:, cols], hid_bf[:, cols, :].rearrange("p o t -> p (o t)"),
            )
            nc.vector.tensor_copy(vs_g[g][:], vs_sb[:].indirect(store_list[:, P // 16 * g : P // 16 * (g + 1)]))

        p_sb = [sbuf("p_sb%d" % h, [P, O], F32) for h in range(halves)]
        first = sbuf("first", [P, halves, U], F32)
        second = sbuf("second", [P, halves, U], F32)
        y = sbuf("y", [P, halves, U], F32)
        for h in range(halves):
            for g, cols in enumerate(reads):
                p_ps = ps.tile([P, P], F32, name="p_ps%d%d" % (g, h))
                nc.tensor.matmul_mx(
                    p_ps[:], lhsT=vs_g[h][:].bitcast(E4M3), lhsT_scale=vs_plane_g[:, P * h : P * (h + 1)],
                    rhs=hid_q[:, cols].bitcast(E5M2), rhs_scale=hid_plane[:, cols], start=True, stop=True,
                )
                if (g, h) == (1, 1):
                    nc.vector.tensor_copy(p_sb[h][:, cols], p_ps[:])
                else:
                    nc.scalar.copy(p_sb[h][:, cols], p_ps[:])
        for h in range(halves):
            nc.vector.tensor_copy(first[:, h, :], p_sb[h][:].indirect(first_list[:]))
            nc.scalar.activation(second[:, h, :], p_sb[h][:].indirect(second_list[:]), ACT.Copy, scale=so_sb[:, h : h + 1])
        for h in range(halves):
            nc.vector.tensor_tensor(y[:, h, :], first[:, h, :], second[:, h, :], ALU.subtract)
            nc.sync.dma_start(out[P * h : P * (h + 1), :], y[:, h, :])
